import numpy as np
import ml_dtypes


def mxq(x, axis, fmt="e4m3"):
    dtype, down = {"e4m3": (ml_dtypes.float8_e4m3fn, 7), "e5m2": (ml_dtypes.float8_e5m2, 14)}[fmt]
    v = np.moveaxis(np.asarray(x, np.float32).astype(ml_dtypes.bfloat16).astype(np.float64), axis, -1)
    blocks = v.reshape(v.shape[:-1] + (-1, 32))
    amax = np.abs(blocks).max(-1, keepdims=True)
    byte = np.maximum(np.where(amax > 0, np.frexp(amax)[1] - 1 + 127, 0) - down, 1)
    scale = np.exp2(byte - 127.0)
    codes = (blocks / scale).astype(np.float32).astype(dtype).astype(np.float64)
    return np.moveaxis((codes * scale).reshape(v.shape), -1, axis)


WIDE = False


def mx_kscale(k):
    if not WIDE:
        return np.ones(k)
    levels = np.array([10, -10, 5, -5, 0])
    if k % 512:
        return np.exp2(np.random.permutation(np.resize(levels, k // 32))).repeat(32)
    a = np.empty((k // 512, 16))
    for p in range(k // 512):
        a[p, :8] = np.random.permutation(np.resize(levels, 8))
        for g in range(8):
            far = levels[np.abs(levels - a[p, g]) >= 10]
            a[p, g + 8] = far[np.random.randint(len(far))]
    return np.exp2(a.ravel()).repeat(32)


def f64(x):
    return np.asarray(x).astype(np.float64)


def striped(idx):
    return np.tile(idx.reshape(-1, 16).T, (8, 1)).astype(np.uint16)


def unstriped(offs):
    return offs[:16].T.reshape(-1).astype(np.int64)


def relu2(v):
    return np.maximum(v, 0.0) ** 2


K, T, S, N = 512, 1024, 512, 256


def setup_inputs():
    n = np.random.standard_normal
    s = mx_kscale(K)[:, None]
    return {
        "xT": (n((K, T)) * s).astype(np.float32),
        "w": (n((K, N)) / np.sqrt(K) / s).astype(np.float32),
        "b": (0.3 * n((N, 1))).astype(np.float32),
        "offs": striped(np.sort(np.random.permutation(T)[:S])),
    }


def reference(xT, w, b, offs):
    idx = unstriped(offs)
    xq = mxq(f64(xT)[:, idx], 0, "e4m3")
    y = mxq(f64(w), 0, "e4m3").T @ xq
    y = relu2(y + f64(b))
    return y

@@ -1,0 +1,177 @@
+from contextlib import ExitStack
+
+import concourse.mybir as mybir
+
+K, T, S, N = 512, 1024, 512, 256
+P = 128
+FLOPS = 2 * K * N * S
+
+F32 = mybir.dt.float32
+BF16 = mybir.dt.bfloat16
+U32 = mybir.dt.uint32
+U16 = mybir.dt.uint16
+U8 = mybir.dt.uint8
+FP8X4 = mybir.dt.float8_e4m3fn_x4
+ADD, MAX, MULT = mybir.AluOpType.add, mybir.AluOpType.max, mybir.AluOpType.mult
+RELU = mybir.ActivationFunctionType.Relu
+SQUARE = mybir.ActivationFunctionType.Square
+
+
+def tile_picked_pick_lin_relu2_srt_e_kernel(tc, xT, w, b, offs, out):
+    nc = tc.nc
+    with ExitStack() as ctx:
+        keep = ctx.enter_context(tc.tile_pool(name="keep", bufs=1))
+        psum = ctx.enter_context(tc.psum_pool(name="psum", bufs=1))
+
+        x_rows = xT.rearrange("(p j) t -> p j t", j=4)
+        out_rows = out.rearrange("(m p) s -> p m s", m=2)
+        V, A = nc.vector.tensor_copy, nc.scalar.copy
+
+        offs_sb = keep.tile([P, S // 16], U16, name="offs_sb")
+        w_raw = keep.tile([P, 4, N], F32, name="w_raw")
+        b_sb = keep.tile([P, 2], F32, name="b_sb")
+        chunks = []
+        quads = []
+
+        def load_x(us, t0, t1):
+            rows = keep.tile([P, 2 * len(us), t1 - t0], F32, name=f"x{us[0]}_{t0}")
+            nc.sync.dma_start(out=rows[:], in_=x_rows[:, 2 * us[0] : 2 * us[-1] + 2, t0:t1])
+            for i, u in enumerate(us):
+                chunks.append((u, t0, t1, rows[:, 2 * i : 2 * i + 2, :]))
+            if len(us) == 2:
+                quads.append((chunks[-2], chunks[-1], rows))
+
+        def load_w():
+            nc.sync.dma_start(out=w_raw[:], in_=w.rearrange("(p j) n -> p j n", j=4))
+
+        def load_offs():
+            nc.sync.dma_start(offs_sb[:], offs)
+
+        def load_b():
+            nc.sync.dma_start(out=b_sb[:], in_=b.rearrange("(m p) o -> p (m o)", m=2))
+
+        load_x((0,), 0, 512)
+        load_x((1,), 0, 512)
+        load_offs()
+        load_x((0, 1), 512, 768)
+        load_x((0, 1), 768, 896)
+        load_w()
+        load_x((0, 1), 896, 1024)
+        load_b()
+
+        zero = keep.tile([P, 1], F32, name="zero")
+        zero2 = keep.tile([P, 1], F32, name="zero2")
+        nc.gpsimd.memset(zero[:], 0.0)
+        nc.scalar.activation(zero2[:], zero[:], RELU)
+
+        w_bf = keep.tile([P, N, 4], BF16, name="w_bf", align_bytes=64)
+        w_codes = keep.tile([P, N], U32, name="w_codes", align_bytes=64)
+        w_scales = keep.tile([P, N], U8, name="w_scales", align_bytes=64)
+
+        def inter_w(engine_copy, c0, c1):
+            engine_copy(
+                out=w_bf[:, c0:c1, :].rearrange("p (c i) j -> p c j i", i=4),
+                in_=w_raw[:, :, c0:c1].rearrange("p j (c i) -> p c j i", i=4),
+            )
+
+        def quantize_w():
+            nc.vector.quantize_mx(out=w_codes[:].bitcast(FP8X4), scales=w_scales[:], in_=w_bf[:].rearrange("p n j -> p (n j)"))
+
+        xp = keep.tile([P, 2, T, 2], BF16, name="xp", align_bytes=64)
+
+        def pairs(engine_copy, u, t0, t1):
+            for cu, c0, c1, rows in chunks:
+                if cu == u and c0 <= t0 and t1 <= c1:
+                    engine_copy(
+                        out=xp[:, u, t0:t1, :],
+                        in_=rows[:, :, t0 - c0 : t1 - c0].rearrange("p e t -> p t e"),
+                    )
+
+        def both(engine_copy, t0, t1):
+            for (cu, c0, c1, rows), (cu2, d0, d1, rows2), src in quads:
+                if c0 <= t0 and t1 <= c1:
+                    engine_copy(
+                        out=xp[:, :, t0:t1, :],
+                        in_=src[:, :, t0 - c0 : t1 - c0].rearrange("p (u e) t -> p u t e", u=2),
+                    )
+
+        words = xp[:].rearrange("p u t e -> p u (t e)").bitcast(U32)
+        state = []
+        for g, (a, z, win) in enumerate(((0, 256, 768), (256, 384, 896), (384, 512, 1024))):
+            n = z - a
+            xg = keep.tile([P, n, 4], BF16, name=f"xg{g}", align_bytes=64)
+            codes = keep.tile([P, n], U32, name=f"codes{g}", align_bytes=64)
+            scales = keep.tile([P, n], U8, name=f"scales{g}", align_bytes=64)
+            acc = [psum.tile([P, n], F32, name=f"acc{g}_{m}") for m in range(2)]
+            r = keep.tile([P, 2, n], F32, name=f"r{g}")
+            o = keep.tile([P, 2, n], F32, name=f"o{g}")
+            state.append((a, z, win, xg, codes, scales, acc, r, o))
+
+        def gather(g, us=(0, 1)):
+            a, z, win, xg = state[g][:4]
+            xg_words = xg[:].rearrange("p n k -> p (n k)").bitcast(U32).rearrange("p (n u) -> p n u", u=2)
+            for u in us:
+                nc.vector.tensor_copy(xg_words[:, :, u], words[:, u, 0:win].indirect(offs_sb[:, a // 16 : z // 16]))
+
+        def quantize(g):
+            xg, codes, scales = state[g][3:6]
+            nc.vector.quantize_mx(out=codes[:].bitcast(FP8X4), scales=scales[:], in_=xg[:].rearrange("p n k -> p (n k)"))
+
+        def multiply(g):
+            codes, scales, acc = state[g][4:7]
+            for m in range(2):
+                cols = slice(m * P, (m + 1) * P)
+                nc.tensor.matmul_mx(
+                    out=acc[m][:],
+                    lhsT=w_codes[:, cols].bitcast(FP8X4),
+                    lhsT_scale=w_scales[:, cols],
+                    rhs=codes[:].bitcast(FP8X4),
+                    rhs_scale=scales[:],
+                    start=True,
+                    stop=True,
+                )
+
+        def finish_scalar(g, ms):
+            acc, r, o = state[g][6:9]
+            for m in ms:
+                nc.scalar.activation(r[:, m, :], acc[m][:], RELU, bias=b_sb[:, m : m + 1])
+            for m in ms:
+                nc.scalar.activation(o[:, m, :], r[:, m, :], SQUARE)
+
+        def finish_vector(g, ms):
+            acc, r, o = state[g][6:9]
+            for m in ms:
+                nc.vector.tensor_scalar(r[:, m, :], acc[m][:], b_sb[:, m : m + 1], 0.0, ADD, MAX)
+            for m in ms:
+                nc.vector.tensor_tensor(o[:, m, :], r[:, m, :], r[:, m, :], MULT)
+
+        def store(g):
+            a, z = state[g][:2]
+            nc.sync.dma_start(out=out_rows[:, :, a:z], in_=state[g][8][:])
+
+        pairs(V, 0, 0, 304)
+        pairs(A, 0, 304, 512)
+        pairs(V, 1, 0, 304)
+        pairs(A, 1, 304, 512)
+        pairs(V, 0, 512, 768)
+        pairs(A, 1, 512, 768)
+        gather(0)
+        both(A, 768, 896)
+        inter_w(A, 0, 256)
+        gather(1)
+        quantize(0)
+        quantize(1)
+        both(A, 896, 1024)
+        quantize_w()
+        multiply(0)
+        multiply(1)
+        gather(2)
+        quantize(2)
+        multiply(2)
+        finish_scalar(0, (0, 1))
+        store(0)
+        finish_vector(1, (0,1))
+        store(1)
+        finish_scalar(2, (0,))
+        finish_vector(2, (1,))
+        store(2)

@@ -31,15 +31,12 @@ def tile_picked_pick_lin_relu2_srt_e_kernel(tc, xT, w, b, offs, out):
         w_raw = keep.tile([P, 4, N], F32, name="w_raw")
         b_sb = keep.tile([P, 2], F32, name="b_sb")
         chunks = []
-        quads = []
 
         def load_x(us, t0, t1):
             rows = keep.tile([P, 2 * len(us), t1 - t0], F32, name=f"x{us[0]}_{t0}")
             nc.sync.dma_start(out=rows[:], in_=x_rows[:, 2 * us[0] : 2 * us[-1] + 2, t0:t1])
             for i, u in enumerate(us):
                 chunks.append((u, t0, t1, rows[:, 2 * i : 2 * i + 2, :]))
-            if len(us) == 2:
-                quads.append((chunks[-2], chunks[-1], rows))
 
         def load_w():
             nc.sync.dma_start(out=w_raw[:], in_=w.rearrange("(p j) n -> p j n", j=4))
@@ -50,13 +47,14 @@ def tile_picked_pick_lin_relu2_srt_e_kernel(tc, xT, w, b, offs, out):
         def load_b():
             nc.sync.dma_start(out=b_sb[:], in_=b.rearrange("(m p) o -> p (m o)", m=2))
 
-        load_x((0,), 0, 512)
-        load_x((1,), 0, 512)
-        load_offs()
-        load_x((0, 1), 512, 768)
-        load_x((0, 1), 768, 896)
         load_w()
-        load_x((0, 1), 896, 1024)
+        load_x((0,), 0, 512)
+        load_x((0,), 512, 768)
+        load_x((0,), 768, 1024)
+        load_offs()
+        load_x((1,), 0, 512)
+        load_x((1,), 512, 768)
+        load_x((1,), 768, 1024)
         load_b()
 
         zero = keep.tile([P, 1], F32, name="zero")
@@ -87,19 +85,12 @@ def tile_picked_pick_lin_relu2_srt_e_kernel(tc, xT, w, b, offs, out):
                         in_=rows[:, :, t0 - c0 : t1 - c0].rearrange("p e t -> p t e"),
                     )
 
-        def both(engine_copy, t0, t1):
-            for (cu, c0, c1, rows), (cu2, d0, d1, rows2), src in quads:
-                if c0 <= t0 and t1 <= c1:
-                    engine_copy(
-                        out=xp[:, :, t0:t1, :],
-                        in_=src[:, :, t0 - c0 : t1 - c0].rearrange("p (u e) t -> p u t e", u=2),
-                    )
-
         words = xp[:].rearrange("p u t e -> p u (t e)").bitcast(U32)
+        xg_all = keep.tile([P, S, 4], BF16, name="xg_all", align_bytes=64)
         state = []
-        for g, (a, z, win) in enumerate(((0, 256, 768), (256, 384, 896), (384, 512, 1024))):
+        for g, (a, z, win) in enumerate(((0, 256, 768), (256, 512, 1024))):
             n = z - a
-            xg = keep.tile([P, n, 4], BF16, name=f"xg{g}", align_bytes=64)
+            xg = xg_all[:, a:z, :]
             codes = keep.tile([P, n], U32, name=f"codes{g}", align_bytes=64)
             scales = keep.tile([P, n], U8, name=f"scales{g}", align_bytes=64)
             acc = [psum.tile([P, n], F32, name=f"acc{g}_{m}") for m in range(2)]
@@ -109,13 +100,17 @@ def tile_picked_pick_lin_relu2_srt_e_kernel(tc, xT, w, b, offs, out):
 
         def gather(g, us=(0, 1)):
             a, z, win, xg = state[g][:4]
-            xg_words = xg[:].rearrange("p n k -> p (n k)").bitcast(U32).rearrange("p (n u) -> p n u", u=2)
+            xg_words = xg.rearrange("p n k -> p (n k)").bitcast(U32).rearrange("p (n u) -> p n u", u=2)
             for u in us:
                 nc.vector.tensor_copy(xg_words[:, :, u], words[:, u, 0:win].indirect(offs_sb[:, a // 16 : z // 16]))
 
+        def gather_all(u, a, z, win):
+            xg_words = xg_all[:, a:z, :].rearrange("p n k -> p (n k)").bitcast(U32).rearrange("p (n u) -> p n u", u=2)
+            nc.vector.tensor_copy(xg_words[:, :, u], words[:, u, 0:win].indirect(offs_sb[:, a // 16 : z // 16]))
+
         def quantize(g):
             xg, codes, scales = state[g][3:6]
-            nc.vector.quantize_mx(out=codes[:].bitcast(FP8X4), scales=scales[:], in_=xg[:].rearrange("p n k -> p (n k)"))
+            nc.vector.quantize_mx(out=codes[:].bitcast(FP8X4), scales=scales[:], in_=xg.rearrange("p n k -> p (n k)"))
 
         def multiply(g):
             codes, scales, acc = state[g][4:7]
@@ -149,29 +144,27 @@ def tile_picked_pick_lin_relu2_srt_e_kernel(tc, xT, w, b, offs, out):
             a, z = state[g][:2]
             nc.sync.dma_start(out=out_rows[:, :, a:z], in_=state[g][8][:])
 
-        pairs(V, 0, 0, 304)
-        pairs(A, 0, 304, 512)
-        pairs(V, 1, 0, 304)
-        pairs(A, 1, 304, 512)
-        pairs(V, 0, 512, 768)
-        pairs(A, 1, 512, 768)
-        gather(0)
-        both(A, 768, 896)
-        inter_w(A, 0, 256)
-        gather(1)
-        quantize(0)
-        quantize(1)
-        both(A, 896, 1024)
+        inter_w(A, 0, 96)
+        inter_w(V, 96, 256)
         quantize_w()
+        pairs(A, 0, 0, 192)
+        pairs(V, 0, 192, 512)
+        pairs(V, 0, 512, 768)
+        pairs(A, 0, 768, 1024)
+        gather(0, (0,))
+        gather(1, (0,))
+        pairs(A, 1, 0, 320)
+        pairs(V, 1, 320, 512)
+        pairs(V, 1, 512, 768)
+        gather(0, (1,))
+        pairs(A, 1, 768, 1024)
+        quantize(0)
         multiply(0)
+        gather(1, (1,))
+        quantize(1)
         multiply(1)
-        gather(2)
-        quantize(2)
-        multiply(2)
         finish_scalar(0, (0, 1))
         store(0)
-        finish_vector(1, (0,1))
+        finish_scalar(1, (0,))
+        finish_vector(1, (1,))
         store(1)
-        finish_scalar(2, (0,))
-        finish_vector(2, (1,))
-        store(2)

@@ -32,11 +32,10 @@ def tile_picked_pick_lin_relu2_srt_e_kernel(tc, xT, w, b, offs, out):
         b_sb = keep.tile([P, 2], F32, name="b_sb")
         chunks = []
 
-        def load_x(us, t0, t1):
-            rows = keep.tile([P, 2 * len(us), t1 - t0], F32, name=f"x{us[0]}_{t0}")
-            nc.sync.dma_start(out=rows[:], in_=x_rows[:, 2 * us[0] : 2 * us[-1] + 2, t0:t1])
-            for i, u in enumerate(us):
-                chunks.append((u, t0, t1, rows[:, 2 * i : 2 * i + 2, :]))
+        def load_x(u, t0, t1):
+            rows = keep.tile([P, 2, t1 - t0], F32, name=f"x{u}_{t0}")
+            nc.sync.dma_start(out=rows[:], in_=x_rows[:, 2 * u : 2 * u + 2, t0:t1])
+            chunks.append((u, t0, t1, rows))
 
         def load_w():
             nc.sync.dma_start(out=w_raw[:], in_=w.rearrange("(p j) n -> p j n", j=4))
@@ -44,18 +43,17 @@ def tile_picked_pick_lin_relu2_srt_e_kernel(tc, xT, w, b, offs, out):
         def load_offs():
             nc.sync.dma_start(offs_sb[:], offs)
 
-        def load_b():
-            nc.sync.dma_start(out=b_sb[:], in_=b.rearrange("(m p) o -> p (m o)", m=2))
+        def load_b(queue):
+            queue.dma_start(out=b_sb[:], in_=b.rearrange("(m p) o -> p (m o)", m=2))
 
+        load_b(nc.scalar)
         load_w()
-        load_x((0,), 0, 512)
-        load_x((0,), 512, 768)
-        load_x((0,), 768, 1024)
+        load_x(0, 0, 512)
+        load_x(0, 512, 1024)
         load_offs()
-        load_x((1,), 0, 512)
-        load_x((1,), 512, 768)
-        load_x((1,), 768, 1024)
-        load_b()
+        load_x(1, 0, 512)
+        load_x(1, 512, 768)
+        load_x(1, 768, 1024)
 
         zero = keep.tile([P, 1], F32, name="zero")
         zero2 = keep.tile([P, 1], F32, name="zero2")
@@ -86,85 +84,89 @@ def tile_picked_pick_lin_relu2_srt_e_kernel(tc, xT, w, b, offs, out):
                     )
 
         words = xp[:].rearrange("p u t e -> p u (t e)").bitcast(U32)
-        xg_all = keep.tile([P, S, 4], BF16, name="xg_all", align_bytes=64)
+        xg = keep.tile([P, S, 4], BF16, name="xg", align_bytes=64)
+        xg_words = xg[:].rearrange("p n k -> p (n k)").bitcast(U32).rearrange("p (n u) -> p n u", u=2)
+        codes = keep.tile([P, S], U32, name="codes", align_bytes=64)
+        scales = keep.tile([P, S], U8, name="scales", align_bytes=64)
+
+        def gather(u, a, z, win):
+            nc.vector.tensor_copy(xg_words[:, a:z, u], words[:, u, 0:win].indirect(offs_sb[:, a // 16 : z // 16]))
+
+        def quantize(a, z):
+            nc.vector.quantize_mx(out=codes[:, a:z].bitcast(FP8X4), scales=scales[:, a:z], in_=xg[:, a:z, :].rearrange("p n k -> p (n k)"))
+
         state = []
-        for g, (a, z, win) in enumerate(((0, 256, 768), (256, 512, 1024))):
-            n = z - a
-            xg = xg_all[:, a:z, :]
-            codes = keep.tile([P, n], U32, name=f"codes{g}", align_bytes=64)
-            scales = keep.tile([P, n], U8, name=f"scales{g}", align_bytes=64)
-            acc = [psum.tile([P, n], F32, name=f"acc{g}_{m}") for m in range(2)]
-            r = keep.tile([P, 2, n], F32, name=f"r{g}")
-            o = keep.tile([P, 2, n], F32, name=f"o{g}")
-            state.append((a, z, win, xg, codes, scales, acc, r, o))
+        for g, (a, z) in enumerate(((0, 256), (256, 384), (384, 512))):
+            acc = [psum.tile([P, z - a], F32, name=f"acc{g}_{m}") for m in range(2)]
+            r = keep.tile([P, 2, z - a], F32, name=f"r{g}")
+            o = keep.tile([P, 2, z - a], F32, name=f"o{g}")
+            state.append((a, z, acc, r, o))
 
-        def gather(g, us=(0, 1)):
-            a, z, win, xg = state[g][:4]
-            xg_words = xg.rearrange("p n k -> p (n k)").bitcast(U32).rearrange("p (n u) -> p n u", u=2)
-            for u in us:
-                nc.vector.tensor_copy(xg_words[:, :, u], words[:, u, 0:win].indirect(offs_sb[:, a // 16 : z // 16]))
-
-        def gather_all(u, a, z, win):
-            xg_words = xg_all[:, a:z, :].rearrange("p n k -> p (n k)").bitcast(U32).rearrange("p (n u) -> p n u", u=2)
-            nc.vector.tensor_copy(xg_words[:, :, u], words[:, u, 0:win].indirect(offs_sb[:, a // 16 : z // 16]))
-
-        def quantize(g):
-            xg, codes, scales = state[g][3:6]
-            nc.vector.quantize_mx(out=codes[:].bitcast(FP8X4), scales=scales[:], in_=xg.rearrange("p n k -> p (n k)"))
-
-        def multiply(g):
-            codes, scales, acc = state[g][4:7]
-            for m in range(2):
+        def multiply(g, a, z, ms=(0, 1)):
+            base, acc = state[g][0], state[g][2]
+            for m in ms:
                 cols = slice(m * P, (m + 1) * P)
                 nc.tensor.matmul_mx(
-                    out=acc[m][:],
+                    out=acc[m][:, a - base : z - base],
                     lhsT=w_codes[:, cols].bitcast(FP8X4),
                     lhsT_scale=w_scales[:, cols],
-                    rhs=codes[:].bitcast(FP8X4),
-                    rhs_scale=scales[:],
+                    rhs=codes[:, a:z].bitcast(FP8X4),
+                    rhs_scale=scales[:, a:z],
                     start=True,
                     stop=True,
                 )
 
-        def finish_scalar(g, ms):
-            acc, r, o = state[g][6:9]
-            for m in ms:
+        def relu(eng, g, m):
+            a, z, acc, r, o = state[g]
+            if eng == "A":
                 nc.scalar.activation(r[:, m, :], acc[m][:], RELU, bias=b_sb[:, m : m + 1])
-            for m in ms:
-                nc.scalar.activation(o[:, m, :], r[:, m, :], SQUARE)
-
-        def finish_vector(g, ms):
-            acc, r, o = state[g][6:9]
-            for m in ms:
+            else:
                 nc.vector.tensor_scalar(r[:, m, :], acc[m][:], b_sb[:, m : m + 1], 0.0, ADD, MAX)
-            for m in ms:
+
+        def square(eng, g, m):
+            a, z, acc, r, o = state[g]
+            if eng == "A":
+                nc.scalar.activation(o[:, m, :], r[:, m, :], SQUARE)
+            else:
                 nc.vector.tensor_tensor(o[:, m, :], r[:, m, :], r[:, m, :], MULT)
 
         def store(g):
-            a, z = state[g][:2]
-            nc.sync.dma_start(out=out_rows[:, :, a:z], in_=state[g][8][:])
+            nc.sync.dma_start(out=out_rows[:, :, state[g][0] : state[g][1]], in_=state[g][4][:])
 
         inter_w(A, 0, 96)
         inter_w(V, 96, 256)
         quantize_w()
         pairs(A, 0, 0, 192)
         pairs(V, 0, 192, 512)
-        pairs(V, 0, 512, 768)
-        pairs(A, 0, 768, 1024)
-        gather(0, (0,))
-        gather(1, (0,))
-        pairs(A, 1, 0, 320)
-        pairs(V, 1, 320, 512)
+        pairs(A, 0, 512, 704)
+        pairs(V, 0, 704, 1024)
+        gather(0, 0, 512, 1024)
+        pairs(A, 1, 0, 384)
+        pairs(V, 1, 384, 512)
         pairs(V, 1, 512, 768)
-        gather(0, (1,))
-        pairs(A, 1, 768, 1024)
-        quantize(0)
-        multiply(0)
-        gather(1, (1,))
-        quantize(1)
-        multiply(1)
-        finish_scalar(0, (0, 1))
+        gather(1, 0, 256, 768)
+        pairs(V, 1, 768, 896)
+        pairs(A, 1, 896, 1024)
+        quantize(0, 256)
+        multiply(0, 0, 256)
+        gather(1, 256, 384, 896)
+        gather(1, 384, 512, 1024)
+        quantize(256, 384)
+        multiply(1, 256, 384)
+        quantize(384, 512)
+        multiply(2, 384, 512)
+        relu("A", 0, 0)
+        relu("A", 0, 1)
+        square("A", 0, 0)
+        square("A", 0, 1)
         store(0)
-        finish_scalar(1, (0,))
-        finish_vector(1, (1,))
+        relu("V", 1, 1)
+        relu("A", 1, 0)
+        square("V", 1, 1)
+        square("A", 1, 0)
         store(1)
+        relu("V", 2, 1)
+        relu("A", 2, 0)
+        square("V", 2, 1)
+        square("A", 2, 0)
+        store(2)

@@ -47,12 +47,11 @@ def tile_picked_pick_lin_relu2_srt_e_kernel(tc, xT, w, b, offs, out):
             queue.dma_start(out=b_sb[:], in_=b.rearrange("(m p) o -> p (m o)", m=2))
 
         load_b(nc.scalar)
-        load_w()
-        load_x(0, 0, 512)
-        load_x(0, 512, 1024)
+        load_x(0, 0, 768)
+        load_x(0, 768, 1024)
         load_offs()
-        load_x(1, 0, 512)
-        load_x(1, 512, 768)
+        load_x(1, 0, 768)
+        load_w()
         load_x(1, 768, 1024)
 
         zero = keep.tile([P, 1], F32, name="zero")
@@ -133,22 +132,21 @@ def tile_picked_pick_lin_relu2_srt_e_kernel(tc, xT, w, b, offs, out):
         def store(g):
             nc.sync.dma_start(out=out_rows[:, :, state[g][0] : state[g][1]], in_=state[g][4][:])
 
-        inter_w(A, 0, 96)
-        inter_w(V, 96, 256)
-        quantize_w()
-        pairs(A, 0, 0, 192)
-        pairs(V, 0, 192, 512)
-        pairs(A, 0, 512, 704)
-        pairs(V, 0, 704, 1024)
-        gather(0, 0, 512, 1024)
-        pairs(A, 1, 0, 384)
-        pairs(V, 1, 384, 512)
-        pairs(V, 1, 512, 768)
+        pairs(A, 0, 0, 256)
+        pairs(V, 0, 256, 768)
+        pairs(A, 0, 768, 1024)
+        gather(0, 0, 256, 768)
+        gather(0, 256, 512, 1024)
+        pairs(A, 1, 0, 272)
+        pairs(V, 1, 272, 768)
         gather(1, 0, 256, 768)
-        pairs(V, 1, 768, 896)
-        pairs(A, 1, 896, 1024)
+        inter_w(A, 0, 160)
+        inter_w(V, 160, 256)
         quantize(0, 256)
+        quantize_w()
         multiply(0, 0, 256)
+        pairs(A, 1, 768, 896)
+        pairs(A, 1, 896, 1024)
         gather(1, 256, 384, 896)
         gather(1, 384, 512, 1024)
         quantize(256, 384)
@@ -156,17 +154,17 @@ def tile_picked_pick_lin_relu2_srt_e_kernel(tc, xT, w, b, offs, out):
         quantize(384, 512)
         multiply(2, 384, 512)
         relu("A", 0, 0)
-        relu("A", 0, 1)
-        square("A", 0, 0)
-        square("A", 0, 1)
-        store(0)
-        relu("V", 1, 1)
+        relu("V", 0, 1)
         relu("A", 1, 0)
-        square("V", 1, 1)
+        relu("V", 1, 1)
+        square("A", 0, 0)
+        square("V", 0, 1)
+        store(0)
         square("A", 1, 0)
+        square("V", 1, 1)
         store(1)
-        relu("V", 2, 1)
         relu("A", 2, 0)
-        square("V", 2, 1)
+        relu("V", 2, 1)
         square("A", 2, 0)
+        square("V", 2, 1)
         store(2)

@@ -129,6 +129,9 @@ def tile_picked_pick_lin_relu2_srt_e_kernel(tc, xT, w, b, offs, out):
             else:
                 nc.vector.tensor_tensor(o[:, m, :], r[:, m, :], r[:, m, :], MULT)
 
+        def store_half(g, m, queue=nc.sync):
+            queue.dma_start(out=out_rows[:, m, state[g][0] : state[g][1]], in_=state[g][4][:, m, :])
+
         def store(g):
             nc.sync.dma_start(out=out_rows[:, :, state[g][0] : state[g][1]], in_=state[g][4][:])
 
@@ -154,17 +157,19 @@ def tile_picked_pick_lin_relu2_srt_e_kernel(tc, xT, w, b, offs, out):
         quantize(384, 512)
         multiply(2, 384, 512)
         relu("A", 0, 0)
-        relu("V", 0, 1)
-        relu("A", 1, 0)
-        relu("V", 1, 1)
         square("A", 0, 0)
-        square("V", 0, 1)
-        store(0)
-        square("A", 1, 0)
+        store_half(0, 0)
+        relu("A", 0, 1)
+        square("A", 0, 1)
+        store_half(0, 1)
+        relu("V", 1, 0)
+        relu("V", 1, 1)
+        square("V", 1, 0)
         square("V", 1, 1)
         store(1)
         relu("A", 2, 0)
         relu("V", 2, 1)
         square("A", 2, 0)
         square("V", 2, 1)
-        store(2)
+        store_half(2, 0)
+        store_half(2, 1)

from contextlib import ExitStack

import concourse.mybir as mybir

K, T, S, N = 512, 1024, 512, 256
P = 128
FLOPS = 2 * K * N * S

F32 = mybir.dt.float32
BF16 = mybir.dt.bfloat16
U32 = mybir.dt.uint32
U16 = mybir.dt.uint16
U8 = mybir.dt.uint8
FP8X4 = mybir.dt.float8_e4m3fn_x4
ADD, MAX, MULT = mybir.AluOpType.add, mybir.AluOpType.max, mybir.AluOpType.mult
RELU = mybir.ActivationFunctionType.Relu
SQUARE = mybir.ActivationFunctionType.Square


def tile_picked_pick_lin_relu2_srt_e_kernel(tc, xT, w, b, offs, out):
    nc = tc.nc
    with ExitStack() as ctx:
        keep = ctx.enter_context(tc.tile_pool(name="keep", bufs=1))
        psum = ctx.enter_context(tc.psum_pool(name="psum", bufs=1))

        x_rows = xT.rearrange("(p j) t -> p j t", j=4)
        out_rows = out.rearrange("(m p) s -> p m s", m=2)
        V, A = nc.vector.tensor_copy, nc.scalar.copy

        offs_sb = keep.tile([P, S // 16], U16, name="offs_sb")
        w_raw = keep.tile([P, 4, N], F32, name="w_raw")
        b_sb = keep.tile([P, 2], F32, name="b_sb")
        chunks = []

        def load_x(u, t0, t1):
            rows = keep.tile([P, 2, t1 - t0], F32, name=f"x{u}_{t0}")
            nc.sync.dma_start(out=rows[:], in_=x_rows[:, 2 * u : 2 * u + 2, t0:t1])
            chunks.append((u, t0, t1, rows))

        def load_w():
            nc.sync.dma_start(out=w_raw[:], in_=w.rearrange("(p j) n -> p j n", j=4))

        def load_offs():
            nc.sync.dma_start(offs_sb[:], offs)

        def load_b(queue):
            queue.dma_start(out=b_sb[:], in_=b.rearrange("(m p) o -> p (m o)", m=2))

        load_b(nc.scalar)
        load_x(0, 0, 768)
        load_x(0, 768, 1024)
        load_offs()
        load_x(1, 0, 768)
        load_w()
        load_x(1, 768, 1024)

        zero = keep.tile([P, 1], F32, name="zero")
        zero2 = keep.tile([P, 1], F32, name="zero2")
        nc.gpsimd.memset(zero[:], 0.0)
        nc.scalar.activation(zero2[:], zero[:], RELU)

        w_bf = keep.tile([P, N, 4], BF16, name="w_bf", align_bytes=64)
        w_codes = keep.tile([P, N], U32, name="w_codes", align_bytes=64)
        w_scales = keep.tile([P, N], U8, name="w_scales", align_bytes=64)

        def inter_w(engine_copy, c0, c1):
            engine_copy(
                out=w_bf[:, c0:c1, :].rearrange("p (c i) j -> p c j i", i=4),
                in_=w_raw[:, :, c0:c1].rearrange("p j (c i) -> p c j i", i=4),
            )

        def quantize_w():
            nc.vector.quantize_mx(out=w_codes[:].bitcast(FP8X4), scales=w_scales[:], in_=w_bf[:].rearrange("p n j -> p (n j)"))

        xp = keep.tile([P, 2, T, 2], BF16, name="xp", align_bytes=64)

        def pairs(engine_copy, u, t0, t1):
            for cu, c0, c1, rows in chunks:
                if cu == u and c0 <= t0 and t1 <= c1:
                    engine_copy(
                        out=xp[:, u, t0:t1, :],
                        in_=rows[:, :, t0 - c0 : t1 - c0].rearrange("p e t -> p t e"),
                    )

        words = xp[:].rearrange("p u t e -> p u (t e)").bitcast(U32)
        xg = keep.tile([P, S, 4], BF16, name="xg", align_bytes=64)
        xg_words = xg[:].rearrange("p n k -> p (n k)").bitcast(U32).rearrange("p (n u) -> p n u", u=2)
        codes = keep.tile([P, S], U32, name="codes", align_bytes=64)
        scales = keep.tile([P, S], U8, name="scales", align_bytes=64)

        def gather(u, a, z, win):
            nc.vector.tensor_copy(xg_words[:, a:z, u], words[:, u, 0:win].indirect(offs_sb[:, a // 16 : z // 16]))

        def quantize(a, z):
            nc.vector.quantize_mx(out=codes[:, a:z].bitcast(FP8X4), scales=scales[:, a:z], in_=xg[:, a:z, :].rearrange("p n k -> p (n k)"))

        state = []
        for g, (a, z) in enumerate(((0, 256), (256, 384), (384, 512))):
            acc = [psum.tile([P, z - a], F32, name=f"acc{g}_{m}") for m in range(2)]
            r = keep.tile([P, 2, z - a], F32, name=f"r{g}")
            o = keep.tile([P, 2, z - a], F32, name=f"o{g}")
            state.append((a, z, acc, r, o))

        def multiply(g, a, z, ms=(0, 1)):
            base, acc = state[g][0], state[g][2]
            for m in ms:
                cols = slice(m * P, (m + 1) * P)
                nc.tensor.matmul_mx(
                    out=acc[m][:, a - base : z - base],
                    lhsT=w_codes[:, cols].bitcast(FP8X4),
                    lhsT_scale=w_scales[:, cols],
                    rhs=codes[:, a:z].bitcast(FP8X4),
                    rhs_scale=scales[:, a:z],
                    start=True,
                    stop=True,
                )

        def relu(eng, g, m):
            a, z, acc, r, o = state[g]
            if eng == "A":
                nc.scalar.activation(r[:, m, :], acc[m][:], RELU, bias=b_sb[:, m : m + 1])
            else:
                nc.vector.tensor_scalar(r[:, m, :], acc[m][:], b_sb[:, m : m + 1], 0.0, ADD, MAX)

        def square(eng, g, m):
            a, z, acc, r, o = state[g]
            if eng == "A":
                nc.scalar.activation(o[:, m, :], r[:, m, :], SQUARE)
            else:
                nc.vector.tensor_tensor(o[:, m, :], r[:, m, :], r[:, m, :], MULT)

        def store_half(g, m, queue=nc.sync):
            queue.dma_start(out=out_rows[:, m, state[g][0] : state[g][1]], in_=state[g][4][:, m, :])

        def store(g):
            nc.sync.dma_start(out=out_rows[:, :, state[g][0] : state[g][1]], in_=state[g][4][:])

        pairs(A, 0, 0, 256)
        pairs(V, 0, 256, 768)
        pairs(A, 0, 768, 1024)
        gather(0, 0, 256, 768)
        gather(0, 256, 512, 1024)
        pairs(A, 1, 0, 272)
        pairs(V, 1, 272, 768)
        gather(1, 0, 256, 768)
        inter_w(A, 0, 160)
        inter_w(V, 160, 256)
        quantize(0, 256)
        quantize_w()
        multiply(0, 0, 256)
        pairs(A, 1, 768, 896)
        pairs(A, 1, 896, 1024)
        gather(1, 256, 384, 896)
        gather(1, 384, 512, 1024)
        quantize(256, 384)
        multiply(1, 256, 384)
        quantize(384, 512)
        multiply(2, 384, 512)
        relu("A", 0, 0)
        square("A", 0, 0)
        store_half(0, 0)
        relu("A", 0, 1)
        square("A", 0, 1)
        store_half(0, 1)
        relu("V", 1, 0)
        relu("V", 1, 1)
        square("V", 1, 0)
        square("V", 1, 1)
        store(1)
        relu("A", 2, 0)
        relu("V", 2, 1)
        square("A", 2, 0)
        square("V", 2, 1)
        store_half(2, 0)
        store_half(2, 1)
